import numpy as np
import ml_dtypes


def mxq(x, axis, fmt="e4m3"):
    dtype, down = {"e4m3": (ml_dtypes.float8_e4m3fn, 7), "e5m2": (ml_dtypes.float8_e5m2, 14)}[fmt]
    v = np.moveaxis(np.asarray(x, np.float32).astype(ml_dtypes.bfloat16).astype(np.float64), axis, -1)
    blocks = v.reshape(v.shape[:-1] + (-1, 32))
    amax = np.abs(blocks).max(-1, keepdims=True)
    byte = np.maximum(np.where(amax > 0, np.frexp(amax)[1] - 1 + 127, 0) - down, 1)
    scale = np.exp2(byte - 127.0)
    codes = (blocks / scale).astype(np.float32).astype(dtype).astype(np.float64)
    return np.moveaxis((codes * scale).reshape(v.shape), -1, axis)


WIDE = False


def mx_kscale(k):
    if not WIDE:
        return np.ones(k)
    levels = np.array([10, -10, 5, -5, 0])
    if k % 512:
        return np.exp2(np.random.permutation(np.resize(levels, k // 32))).repeat(32)
    a = np.empty((k // 512, 16))
    for p in range(k // 512):
        a[p, :8] = np.random.permutation(np.resize(levels, 8))
        for g in range(8):
            far = levels[np.abs(levels - a[p, g]) >= 10]
            a[p, g + 8] = far[np.random.randint(len(far))]
    return np.exp2(a.ravel()).repeat(32)


def f64(x):
    return np.asarray(x).astype(np.float64)


def striped(idx):
    return np.tile(idx.reshape(-1, 16).T, (8, 1)).astype(np.uint16)


def unstriped(offs):
    return offs[:16].T.reshape(-1).astype(np.int64)


def pack_weight(w):
    k, n = w.shape
    w = f64(np.asarray(w, np.float32).astype(ml_dtypes.bfloat16)).reshape(k // 32, 32, n)
    amax = np.abs(w).max(1)
    byte = np.clip(np.where(amax > 0, np.frexp(amax)[1] - 1 + 127 - 7, 1), 1, 254)
    scaled = (w * np.exp2(127.0 - byte)[:, None, :]).reshape(k, n).astype(np.float32)
    words = np.ascontiguousarray(scaled.reshape(k // 512, 128, 4, n).transpose(0, 1, 3, 2)).astype(ml_dtypes.float8_e4m3fn).view(np.uint8)
    return words, np.ascontiguousarray(byte.astype(np.uint8).reshape(k // 512, 16, n))


def unpack_weight(words, scales):
    g, p, n, _ = words.shape
    vals = np.ascontiguousarray(words).view(ml_dtypes.float8_e4m3fn).astype(np.float64) * np.repeat(np.exp2(scales.astype(np.float64) - 127.0), 8, axis=1)[..., None]
    return vals.transpose(0, 1, 3, 2).reshape(g * 512, n)


def relu(v):
    return np.maximum(v, 0.0)


K, T, S, N, H = 1024, 1024, 512, 128, 512


def setup_inputs():
    n = np.random.standard_normal
    s = mx_kscale(K)[:, None]
    u = mx_kscale(H)
    packed_xT = pack_weight(n((K, T)) * s)
    return {
        "x_words": packed_xT[0],
        "x_scales": packed_xT[1],
        "w1": (n((K, H)) / np.sqrt(K) / s).astype(np.float32),
        "w2": (n((K, H)) / np.sqrt(K) / s).astype(np.float32),
        "vwa": (n((H, S))).astype(np.float32),
        "vwb": (n((H, S))).astype(np.float32),
        "unit": (np.random.uniform(0.6, 1.4, (H, 1)) * u[:, None]).astype(np.float32),
        "w3": (n((H, N)) / np.sqrt(H) / u[:, None]).astype(np.float32),
        "offs": striped(np.random.permutation(T)[:S]),
        "up1": striped(np.random.permutation(S)),
        "up2": striped(np.random.permutation(S)),
    }


def reference(x_words, x_scales, w1, w2, vwa, vwb, unit, w3, offs, up1, up2):
    xq = unpack_weight(x_words, x_scales)[:, unstriped(offs)]
    y = mxq(f64(w1), 0, "e4m3").T @ xq
    act1 = relu(y - 0.2)
    a1 = act1[:, unstriped(up1)]
    edge1 = a1 * f64(vwa)
    a2 = act1[:, unstriped(up2)]
    edge2 = a2 * f64(vwb)
    tot = np.abs(edge1) + np.abs(edge2) + 0.2
    att1 = edge1 / tot
    ys = mxq(f64(w2), 0, "e4m3").T @ xq
    w1s = ys[:, unstriped(up1)]
    infl = att1 * w1s + (edge2 / tot) * ys
    hid = f64(unit) * infl
    return mxq(f64(w3), 0, "e4m3").T @ mxq(hid, 0, "e4m3")

@@ -1,0 +1,281 @@
+from contextlib import ExitStack
+
+import concourse.mybir as mybir
+from concourse.masks import make_identity
+
+K, T, S, N, H = 1024, 1024, 512, 128, 512
+FLOPS = 2 * (2 * K * H * S + H * N * S)
+
+F32 = mybir.dt.float32
+BF16 = mybir.dt.bfloat16
+I32 = mybir.dt.int32
+U32 = mybir.dt.uint32
+U16 = mybir.dt.uint16
+U8 = mybir.dt.uint8
+FP8X4 = mybir.dt.float8_e4m3fn_x4
+ACT = mybir.ActivationFunctionType
+ALU = mybir.AluOpType
+
+P = 128
+PACK = 4
+PASSES = K // (P * PACK)
+TILES = H // P
+JB = S // P
+PAD = 32
+SHIFT = 0.2
+
+
+def tile_picked_ytcoda_infl_p_kernel(tc, x_words, x_scales, w1, w2, vwa, vwb, unit, w3, offs, up1, up2, out):
+    nc = tc.nc
+    with ExitStack() as ctx:
+        keep = ctx.enter_context(tc.tile_pool(name="keep", bufs=1))
+        ring = ctx.enter_context(tc.tile_pool(name="ring", bufs=2))
+        psum = ctx.enter_context(tc.psum_pool(name="psum", bufs=1))
+
+        offs_sb = keep.tile([P, S // 16], U16, name="offs_sb")
+        up1_sb = keep.tile([P, S // 16], U16, name="up1_sb")
+        up2_sb = keep.tile([P, S // 16], U16, name="up2_sb")
+        x_table = [keep.tile([P, T], U32, name="x_table%d" % g, align_bytes=64) for g in range(PASSES)]
+        scale_table = keep.tile([P, T], U8, name="scale_table", align_bytes=64)
+        x_codes = [keep.tile([P, S], U32, name="x_codes%d" % g, align_bytes=64) for g in range(PASSES)]
+        x_planes = keep.tile([P, S], U8, name="x_planes", align_bytes=64)
+        ident = keep.tile([P, P], F32, name="ident")
+        unit_sb = keep.tile([P, TILES], F32, name="unit_sb")
+        w3_raw = keep.tile([P, PACK, N], F32, name="w3_raw")
+        raw = {}
+        for name in ("w1", "w2"):
+            for t in range(TILES):
+                raw[name, t] = keep.tile([P, PASSES, PACK, P], F32, name="raw_%s_%d" % (name, t))
+        vwa_sb = [keep.tile([P, S], F32, name="vwa%d" % t) for t in range(TILES)]
+        vwb_sb = [keep.tile([P, S], F32, name="vwb%d" % t) for t in range(TILES)]
+        act = [keep.tile([P, S + PAD], F32, name="act%d" % t) for t in range(TILES)]
+        score = [keep.tile([P, S + PAD], F32, name="score%d" % t) for t in range(TILES)]
+        hid_t = keep.tile([P, JB, H], BF16, name="hid_t", align_bytes=64)
+
+        nc.gpsimd.memset(scale_table[:].bitcast(I32), 0)
+
+        def load_words(g):
+            nc.sync.dma_start(out=x_table[g][:].bitcast(I32), in_=x_words[g].rearrange("p n t -> p (n t)").bitcast(I32))
+
+        def load_weight(name, w, t):
+            for g in range(PASSES):
+                rows = w[g * P * PACK : (g + 1) * P * PACK, t * P : (t + 1) * P]
+                nc.sync.dma_start(out=raw[name, t][:, g, :, :], in_=rows.rearrange("(p j) c -> p j c", j=PACK))
+
+        def load_edges(t):
+            nc.sync.dma_start(out=vwa_sb[t][:], in_=vwa[t * P : (t + 1) * P, :])
+            nc.sync.dma_start(out=vwb_sb[t][:], in_=vwb[t * P : (t + 1) * P, :])
+
+        def load_scales():
+            for q in range(4):
+                nc.sync.dma_start(
+                    out=scale_table[32 * q : 32 * q + 4 * PASSES, :].bitcast(I32),
+                    in_=x_scales[:, 4 * q : 4 * q + 4, :].bitcast(I32),
+                )
+
+        def load_unit():
+            with nc.allow_non_contiguous_dma(reason="one value a partition"):
+                nc.sync.dma_start(out=unit_sb[:], in_=unit.rearrange("(t p) o -> p (t o)", p=P))
+
+        def load_list(tile, src):
+            nc.sync.dma_start(tile[:], src)
+
+        load_list(offs_sb, offs)
+        load_scales()
+        load_words(0)
+        load_weight("w1", w1, 0)
+        load_words(1)
+        load_weight("w2", w2, 0)
+        load_list(up1_sb, up1)
+        load_edges(0)
+        load_list(up2_sb, up2)
+        load_unit()
+        load_weight("w1", w1, 1)
+        load_weight("w2", w2, 1)
+        load_weight("w1", w1, 2)
+        load_edges(1)
+        load_weight("w2", w2, 2)
+        load_weight("w1", w1, 3)
+        load_weight("w2", w2, 3)
+        load_edges(2)
+        load_edges(3)
+        nc.sync.dma_start(out=w3_raw[:], in_=w3.rearrange("(p j) c -> p j c", j=PACK))
+
+        make_identity(nc, ident[:])
+        for t in range(TILES):
+            nc.gpsimd.memset(act[t][:, S:], 0.0)
+            nc.gpsimd.memset(score[t][:, S:], 0.0)
+
+        def pick(dst, table):
+            nc.vector.tensor_copy(dst[:], table[:].indirect(offs_sb[:]))
+
+        def quantise(name, t, copy):
+            if (name, t) in host:
+                grouped = host[name, t].bitcast(BF16).rearrange("p (g c j) -> p g c j", g=PASSES, j=PACK)
+            else:
+                grouped = ring.tile([P, PASSES, P, PACK], BF16, name="grouped", align_bytes=64, bufs=4)
+            copy(
+                grouped[:].rearrange("p g (c i) j -> p g c j i", i=4),
+                raw[name, t][:].rearrange("p g j (c i) -> p g c j i", i=4),
+            )
+            codes = keep.tile([P, PASSES * P], U32, name="codes_%s_%d" % (name, t), align_bytes=64)
+            planes = keep.tile([P, PASSES * P], U8, name="planes_%s_%d" % (name, t), align_bytes=64)
+            nc.vector.quantize_mx(out=codes[:].bitcast(FP8X4), scales=planes[:], in_=grouped[:].rearrange("p g c j -> p (g c j)"))
+            quantised[name, t] = (codes, planes)
+
+        def product(name, t):
+            codes, planes = quantised[name, t]
+            acc = psum.tile([P, S], F32, name="acc_" + name)
+            for g in range(PASSES):
+                nc.tensor.matmul_mx(
+                    out=acc[:],
+                    lhsT=codes[:, g * P : (g + 1) * P].bitcast(FP8X4),
+                    lhsT_scale=planes[:, g * P : (g + 1) * P],
+                    rhs=x_codes[g][:].bitcast(FP8X4),
+                    rhs_scale=x_planes[4 * g :, :],
+                    start=(g == 0),
+                    stop=(g == PASSES - 1),
+                )
+            return acc
+
+        def make_act(t):
+            acc = product("w1", t)
+            nc.scalar.activation(act[t][:, :S], acc[:], ACT.Relu, bias=-SHIFT)
+
+        def make_score(t):
+            acc = product("w2", t)
+            nc.scalar.activation(score[t][:, :S], acc[:], ACT.Copy, scale=unit_sb[:, t : t + 1])
+
+        def add_turned(bank, a, b, blocks):
+            for jb in range(blocks):
+                cols = slice(jb * P, (jb + 1) * P)
+                nc.tensor.matmul(bank[:, jb, :], lhsT=a[:, cols], rhs=ident[:], start=True, stop=False, is_transpose=True)
+                nc.tensor.matmul(bank[:, jb, :], lhsT=b[:, cols], rhs=ident[:], start=False, stop=True, is_transpose=True)
+
+        def edges(t, b0, b1):
+            n = (b1 - b0) * P
+            edge = edge_tiles[t][:, :, b0 * P : b1 * P]
+            nc.vector.tensor_tensor(edge[:, 0, :], act[t][:].indirect(up1_sb[:, 8 * b0 : 8 * b1]), vwa_sb[t][:, b0 * P : b1 * P], ALU.mult)
+            nc.vector.tensor_tensor(edge[:, 1, :], act[t][:].indirect(up2_sb[:, 8 * b0 : 8 * b1]), vwb_sb[t][:, b0 * P : b1 * P], ALU.mult)
+            state[t, b0, "edge"] = edge
+
+        def sizes(t, b0, b1):
+            n = (b1 - b0) * P
+            size = ring.tile([P, 2, n], F32, name="size", bufs=3)
+            nc.scalar.activation(size[:], state[t, b0, "edge"][:], ACT.Abs)
+            tot = psum.tile([P, b1 - b0, P], F32, name="tot", bufs=2)
+            add_turned(tot, size[:, 0, :], size[:, 1, :], b1 - b0)
+            state[t, b0, "tot"] = tot
+
+        def invert(t, b0, b1):
+            n = (b1 - b0) * P
+            square = ring.tile([P, n], F32, name="square")
+            nc.scalar.activation(square[:], state[t, b0, "tot"][:].rearrange("p b i -> p (b i)"), ACT.Square, bias=SHIFT)
+            inverse = ring.tile([P, b1 - b0, P], F32, name="inverse", bufs=3)
+            nc.scalar.activation(inverse[:].rearrange("p b i -> p (b i)"), square[:], ACT.Abs_reciprocal_sqrt)
+            state[t, b0, "inverse"] = inverse
+
+        def carried(t, b0, b1):
+            n = (b1 - b0) * P
+            edge = state[t, b0, "edge"]
+            term = terms[t][:, :, b0 * P : b1 * P]
+            nc.vector.tensor_tensor(term[:, 1, :], score[t][:, b0 * P : b1 * P], edge[:, 1, :], ALU.mult)
+            nc.vector.tensor_tensor(term[:, 0, :], score[t][:].indirect(up1_sb[:, 8 * b0 : 8 * b1]), edge[:, 0, :], ALU.mult)
+            num = psum.tile([P, b1 - b0, P], F32, name="num", bufs=2)
+            add_turned(num, term[:, 0, :], term[:, 1, :], b1 - b0)
+            state[t, b0, "num"] = num
+
+        def finish(t, b0, b1):
+            nc.vector.tensor_tensor(hid_t[:, b0:b1, t * P : (t + 1) * P], state[t, b0, "num"][:], state[t, b0, "inverse"][:], ALU.mult)
+
+        def quantise_w3():
+            w3_grouped = keep.tile([P, N, PACK], BF16, name="w3_grouped", align_bytes=64)
+            nc.scalar.copy(
+                w3_grouped[:].rearrange("p (c i) j -> p c j i", i=4), w3_raw[:].rearrange("p j (c i) -> p c j i", i=4)
+            )
+            nc.vector.quantize_mx(out=w3_codes[:].bitcast(FP8X4), scales=w3_planes[:], in_=w3_grouped[:].rearrange("p c j -> p (c j)"))
+
+        def logits(b0, b1, copy, acc_name, evac):
+            nb = b1 - b0
+            n = nb * P
+            hid_words = hid_t[:].bitcast(F32)
+            back = psum.tile([P, nb, 2, P], F32, name="back", bufs=2)
+            for b in range(nb):
+                for u in range(2):
+                    nc.tensor.transpose(back[:, b, u, :], hid_words[:, b0 + b, u : H // 2 : 2], ident[:])
+            hid_grouped = keep.tile([P, n, PACK], BF16, name="hid_grouped%d" % b0, align_bytes=64)
+            words = hid_grouped[:].bitcast(F32).rearrange("p (b j) u -> p b j u", b=nb)
+            copy(words, back[:].rearrange("p b u j -> p b j u"))
+            hid_codes = keep.tile([P, n], U32, name="hid_codes%d" % b0, align_bytes=64)
+            hid_planes = keep.tile([P, n], U8, name="hid_planes%d" % b0, align_bytes=64)
+            nc.vector.quantize_mx(out=hid_codes[:].bitcast(FP8X4), scales=hid_planes[:], in_=hid_grouped[:].rearrange("p c j -> p (c j)"))
+            acc = psum.tile([P, S], F32, name=acc_name)
+            nc.tensor.matmul_mx(
+                out=acc[:, :n],
+                lhsT=w3_codes[:].bitcast(FP8X4),
+                lhsT_scale=w3_planes[:],
+                rhs=hid_codes[:].bitcast(FP8X4),
+                rhs_scale=hid_planes[:],
+                start=True,
+                stop=True,
+            )
+            result = keep.tile([P, n], F32, name="result%d" % b0)
+            evac(result[:], acc[:, :n])
+            nc.sync.dma_start(out=out[:, b0 * P : b1 * P], in_=result[:])
+
+        w3_codes = keep.tile([P, N], U32, name="w3_codes", align_bytes=64)
+        w3_planes = keep.tile([P, N], U8, name="w3_planes", align_bytes=64)
+        terms = [keep.tile([P, 2, S], F32, name="term%d" % t, align_bytes=64) for t in range(TILES)]
+        edge_tiles = [keep.tile([P, 2, S], F32, name="edge%d" % t, align_bytes=64) for t in range(TILES)]
+        host = {("w1", 1): terms[0][:, 1, :], ("w2", 1): terms[0][:, 0, :], ("w1", 2): terms[1][:, 1, :], ("w2", 2): terms[1][:, 0, :], ("w1", 3): terms[2][:, 1, :], ("w2", 3): terms[2][:, 0, :]}
+        quantised = {}
+        state = {}
+        V = nc.vector.tensor_copy
+        A = nc.scalar.copy
+        pick(x_planes, scale_table)
+        pick(x_codes[0], x_table[0])
+        quantise("w1",0,A)
+        pick(x_codes[1], x_table[1])
+        make_act(0)
+        quantise("w2",0,A)
+        make_score(0)
+        quantise("w1",1,A)
+        make_act(1)
+        quantise("w2",1,A)
+        make_score(1)
+        edges(0,0,4)
+        carried(0,0,4)
+        quantise("w1",2,A)
+        make_act(2)
+        sizes(0,0,4)
+        quantise("w2",2,A)
+        make_score(2)
+        edges(1,0,4)
+        carried(1,0,4)
+        invert(0,0,4)
+        quantise("w1",3,A)
+        make_act(3)
+        sizes(1,0,4)
+        quantise("w2",3,A)
+        make_score(3)
+        edges(2,0,4)
+        finish(0,0,4)
+        carried(2,0,4)
+        invert(1,0,4)
+        sizes(2,0,4)
+        edges(3,0,2)
+        finish(1,0,4)
+        invert(2,0,4)
+        quantise_w3()
+        sizes(3,0,2)
+        carried(3,0,2)
+        invert(3,0,2)
+        edges(3,2,4)
+        finish(2,0,4)
+        sizes(3,2,4)
+        finish(3,0,2)
+        carried(3,2,4)
+        logits(0,2,A,"acc_w1",A)
+        invert(3,2,4)
+        finish(3,2,4)
+        logits(2,4,A,"acc_w2",A)

@@ -92,15 +92,18 @@ def tile_picked_ytcoda_infl_p_kernel(tc, x_words, x_scales, w1, w2, vwa, vwb, un
         load_unit()
         load_weight("w1", w1, 1)
         load_weight("w2", w2, 1)
-        load_weight("w1", w1, 2)
         load_edges(1)
+        load_weight("w1", w1, 2)
         load_weight("w2", w2, 2)
+        load_edges(2)
         load_weight("w1", w1, 3)
         load_weight("w2", w2, 3)
-        load_edges(2)
         load_edges(3)
         nc.sync.dma_start(out=w3_raw[:], in_=w3.rearrange("(p j) c -> p j c", j=PACK))
 
+        warm = keep.tile([P, 2], F32, name="warm")
+        nc.gpsimd.memset(warm[:, 0:1], 1.0)
+        nc.scalar.activation(warm[:, 1:2], warm[:, 0:1], ACT.Abs_reciprocal_sqrt)
         make_identity(nc, ident[:])
         for t in range(TILES):
             nc.gpsimd.memset(act[t][:, S:], 0.0)
@@ -120,6 +123,18 @@ def tile_picked_ytcoda_infl_p_kernel(tc, x_words, x_scales, w1, w2, vwa, vwb, un
             )
             codes = keep.tile([P, PASSES * P], U32, name="codes_%s_%d" % (name, t), align_bytes=64)
             planes = keep.tile([P, PASSES * P], U8, name="planes_%s_%d" % (name, t), align_bytes=64)
+            nc.vector.quantize_mx(out=codes[:].bitcast(FP8X4), scales=planes[:], in_=grouped[:].rearrange("p g c j -> p (g c j)"))
+            quantised[name, t] = (codes, planes)
+
+        def quantise_by_pass(name, t, copy):
+            codes = keep.tile([P, PASSES * P], U32, name="codes_%s_%d" % (name, t), align_bytes=64)
+            planes = keep.tile([P, PASSES * P], U8, name="planes_%s_%d" % (name, t), align_bytes=64)
+            grouped = ring.tile([P, PASSES, P, PACK], BF16, name="grouped", align_bytes=64, bufs=4)
+            for g in range(PASSES):
+                copy(
+                    grouped[:, g, :, :].rearrange("p (c i) j -> p c j i", i=4),
+                    raw[name, t][:, g, :, :].rearrange("p j (c i) -> p c j i", i=4),
+                )
             nc.vector.quantize_mx(out=codes[:].bitcast(FP8X4), scales=planes[:], in_=grouped[:].rearrange("p g c j -> p (g c j)"))
             quantised[name, t] = (codes, planes)
 
@@ -152,12 +167,37 @@ def tile_picked_ytcoda_infl_p_kernel(tc, x_words, x_scales, w1, w2, vwa, vwb, un
                 nc.tensor.matmul(bank[:, jb, :], lhsT=a[:, cols], rhs=ident[:], start=True, stop=False, is_transpose=True)
                 nc.tensor.matmul(bank[:, jb, :], lhsT=b[:, cols], rhs=ident[:], start=False, stop=True, is_transpose=True)
 
-        def edges(t, b0, b1):
-            n = (b1 - b0) * P
+        def fetch(name, table, order, t, b0, b1):
+            got = keep.tile([P, (b1 - b0) * P], F32, name="%s_%d_%d" % (name, t, b0))
+            nc.scalar.activation(got[:], table[t][:].indirect(order[:, 8 * b0 : 8 * b1]), ACT.Copy)
+            state[t, b0, name] = got
+
+        def fetch2(t, b0, b1):
+            fetch("a2", act, up2_sb, t, b0, b1)
+
+        def fetch1(t, b0, b1):
+            fetch("a1", act, up1_sb, t, b0, b1)
+
+        def fetch3(t, b0, b1):
+            fetch("w1s", score, up1_sb, t, b0, b1)
+
+        def looked(name, table, order, t, b0, b1):
+            if (t, b0, name) in state:
+                return state[t, b0, name][:]
+            return table[t][:].indirect(order[:, 8 * b0 : 8 * b1])
+
+        def edge1(t, b0, b1):
             edge = edge_tiles[t][:, :, b0 * P : b1 * P]
-            nc.vector.tensor_tensor(edge[:, 0, :], act[t][:].indirect(up1_sb[:, 8 * b0 : 8 * b1]), vwa_sb[t][:, b0 * P : b1 * P], ALU.mult)
-            nc.vector.tensor_tensor(edge[:, 1, :], act[t][:].indirect(up2_sb[:, 8 * b0 : 8 * b1]), vwb_sb[t][:, b0 * P : b1 * P], ALU.mult)
+            nc.vector.tensor_tensor(edge[:, 0, :], looked("a1", act, up1_sb, t, b0, b1), vwa_sb[t][:, b0 * P : b1 * P], ALU.mult)
             state[t, b0, "edge"] = edge
+
+        def edge2(t, b0, b1):
+            edge = edge_tiles[t][:, :, b0 * P : b1 * P]
+            nc.vector.tensor_tensor(edge[:, 1, :], looked("a2", act, up2_sb, t, b0, b1), vwb_sb[t][:, b0 * P : b1 * P], ALU.mult)
+
+        def edges(t, b0, b1):
+            edge1(t, b0, b1)
+            edge2(t, b0, b1)
 
         def sizes(t, b0, b1):
             n = (b1 - b0) * P
@@ -180,7 +220,7 @@ def tile_picked_ytcoda_infl_p_kernel(tc, x_words, x_scales, w1, w2, vwa, vwb, un
             edge = state[t, b0, "edge"]
             term = terms[t][:, :, b0 * P : b1 * P]
             nc.vector.tensor_tensor(term[:, 1, :], score[t][:, b0 * P : b1 * P], edge[:, 1, :], ALU.mult)
-            nc.vector.tensor_tensor(term[:, 0, :], score[t][:].indirect(up1_sb[:, 8 * b0 : 8 * b1]), edge[:, 0, :], ALU.mult)
+            nc.vector.tensor_tensor(term[:, 0, :], looked("w1s", score, up1_sb, t, b0, b1), edge[:, 0, :], ALU.mult)
             num = psum.tile([P, b1 - b0, P], F32, name="num", bufs=2)
             add_turned(num, term[:, 0, :], term[:, 1, :], b1 - b0)
             state[t, b0, "num"] = num
@@ -190,7 +230,7 @@ def tile_picked_ytcoda_infl_p_kernel(tc, x_words, x_scales, w1, w2, vwa, vwb, un
 
         def quantise_w3():
             w3_grouped = keep.tile([P, N, PACK], BF16, name="w3_grouped", align_bytes=64)
-            nc.scalar.copy(
+            nc.vector.tensor_copy(
                 w3_grouped[:].rearrange("p (c i) j -> p c j i", i=4), w3_raw[:].rearrange("p j (c i) -> p c j i", i=4)
             )
             nc.vector.quantize_mx(out=w3_codes[:].bitcast(FP8X4), scales=w3_planes[:], in_=w3_grouped[:].rearrange("p c j -> p (c j)"))
@@ -227,55 +267,71 @@ def tile_picked_ytcoda_infl_p_kernel(tc, x_words, x_scales, w1, w2, vwa, vwb, un
         w3_planes = keep.tile([P, N], U8, name="w3_planes", align_bytes=64)
         terms = [keep.tile([P, 2, S], F32, name="term%d" % t, align_bytes=64) for t in range(TILES)]
         edge_tiles = [keep.tile([P, 2, S], F32, name="edge%d" % t, align_bytes=64) for t in range(TILES)]
-        host = {("w1", 1): terms[0][:, 1, :], ("w2", 1): terms[0][:, 0, :], ("w1", 2): terms[1][:, 1, :], ("w2", 2): terms[1][:, 0, :], ("w1", 3): terms[2][:, 1, :], ("w2", 3): terms[2][:, 0, :]}
+        host = { }
         quantised = {}
         state = {}
         V = nc.vector.tensor_copy
         A = nc.scalar.copy
         pick(x_planes, scale_table)
         pick(x_codes[0], x_table[0])
-        quantise("w1",0,A)
+        quantise_by_pass("w1",0,A)
         pick(x_codes[1], x_table[1])
         make_act(0)
-        quantise("w2",0,A)
+        quantise("w2",0,V)
         make_score(0)
-        quantise("w1",1,A)
+        edge1(0,0,4)
+        fetch2(0,0,4)
+        fetch3(0,0,4)
+        quantise("w1",1,V)
         make_act(1)
-        quantise("w2",1,A)
+        edge2(0,0,4)
+        quantise("w2",1,V)
         make_score(1)
-        edges(0,0,4)
         carried(0,0,4)
-        quantise("w1",2,A)
-        make_act(2)
         sizes(0,0,4)
-        quantise("w2",2,A)
-        make_score(2)
-        edges(1,0,4)
-        carried(1,0,4)
+        edge1(1,0,4)
+        fetch2(1,0,4)
+        fetch3(1,0,4)
+        quantise("w1",2,V)
+        make_act(2)
+        edge2(1,0,4)
         invert(0,0,4)
-        quantise("w1",3,A)
-        make_act(3)
+        quantise("w2",2,V)
+        make_score(2)
+        carried(1,0,4)
         sizes(1,0,4)
-        quantise("w2",3,A)
-        make_score(3)
-        edges(2,0,4)
         finish(0,0,4)
-        carried(2,0,4)
+        edge1(2,0,4)
+        fetch2(2,0,4)
+        fetch3(2,0,4)
+        quantise("w1",3,V)
+        make_act(3)
+        edge2(2,0,4)
         invert(1,0,4)
+        quantise("w2",3,V)
+        make_score(3)
+        carried(2,0,4)
         sizes(2,0,4)
-        edges(3,0,2)
         finish(1,0,4)
+        edges(3,0,2)
         invert(2,0,4)
         quantise_w3()
         sizes(3,0,2)
+        fetch3(3,0,2)
+        edges(3,2,3)
         carried(3,0,2)
         invert(3,0,2)
-        edges(3,2,4)
+        sizes(3,2,3)
+        edges(3,3,4)
         finish(2,0,4)
-        sizes(3,2,4)
         finish(3,0,2)
-        carried(3,2,4)
+        invert(3,2,3)
+        carried(3,2,3)
+        sizes(3,3,4)
         logits(0,2,A,"acc_w1",A)
-        invert(3,2,4)
-        finish(3,2,4)
-        logits(2,4,A,"acc_w2",A)
+        carried(3,3,4)
+        invert(3,3,4)
+        finish(3,2,3)
+        finish(3,3,4)
+        logits(2,3,A,"acc_w2",A)
+        logits(3,4,A,"acc_w1",A)

@@ -23,6 +23,8 @@ TILES = H // P
 JB = S // P
 PAD = 32
 SHIFT = 0.2
+SLAB = PACK * P
+BUFS = {"num": 2, "tot": 2, "back": 2, "acc_w1": 1, "acc_w2": 1}
 
 
 def tile_picked_ytcoda_infl_p_kernel(tc, x_words, x_scales, w1, w2, vwa, vwb, unit, w3, offs, up1, up2, out):
@@ -40,30 +42,54 @@ def tile_picked_ytcoda_infl_p_kernel(tc, x_words, x_scales, w1, w2, vwa, vwb, un
         x_codes = [keep.tile([P, S], U32, name="x_codes%d" % g, align_bytes=64) for g in range(PASSES)]
         x_planes = keep.tile([P, S], U8, name="x_planes", align_bytes=64)
         ident = keep.tile([P, P], F32, name="ident")
+        unit_rows = keep.tile([P, P], F32, name="unit_rows")
         unit_sb = keep.tile([P, TILES], F32, name="unit_sb")
-        w3_raw = keep.tile([P, PACK, N], F32, name="w3_raw")
-        raw = {}
-        for name in ("w1", "w2"):
-            for t in range(TILES):
-                raw[name, t] = keep.tile([P, PASSES, PACK, P], F32, name="raw_%s_%d" % (name, t))
         vwa_sb = [keep.tile([P, S], F32, name="vwa%d" % t) for t in range(TILES)]
         vwb_sb = [keep.tile([P, S], F32, name="vwb%d" % t) for t in range(TILES)]
         act = [keep.tile([P, S + PAD], F32, name="act%d" % t) for t in range(TILES)]
         score = [keep.tile([P, S + PAD], F32, name="score%d" % t) for t in range(TILES)]
         hid_t = keep.tile([P, JB, H], BF16, name="hid_t", align_bytes=64)
 
+        groups = [[("w1", 0)], [("w1", 1)], [("w2", 0)], [("w1", 2), ("w2", 1)], [("w1", 3), ("w2", 2)], [("w2", 3), ("w3", 0)]]
+        source = {"w1": w1, "w2": w2, "w3": w3}
+        raw, codes, planes, place = [], [], [], {}
+        for n, group in enumerate(groups):
+            slabs = 0
+            for name, t in group:
+                place[name, t] = (n, slabs)
+                slabs = slabs + source[name].shape[0] // SLAB
+            raw.append(keep.tile([P, slabs, SLAB], F32, name="raw_%d" % n, align_bytes=64))
+            codes.append(keep.tile([P, slabs * P], U32, name="codes%d" % n, align_bytes=64))
+            planes.append(keep.tile([P, slabs * P], U8, name="planes%d" % n, align_bytes=64))
+
+        def home(name, t):
+            n, s0 = place[name, t]
+            return raw[n][:, s0 : s0 + PASSES, :]
+
+        edge = [home("w1", 1), home("w1", 2), home("w1", 3), home("w2", 3)]
+        term = [home("w2", 1), home("w2", 2), home("w1", 0), home("w2", 0)]
+
         nc.gpsimd.memset(scale_table[:].bitcast(I32), 0)
+        nc.gpsimd.memset(unit_rows[:], 0.0)
+        warm = keep.tile([P, 2], F32, name="warm")
+        nc.gpsimd.memset(warm[:, 0:1], 1.0)
+        nc.scalar.activation(warm[:, 1:2], warm[:, 0:1], ACT.Abs_reciprocal_sqrt)
 
         def load_words(g):
             nc.sync.dma_start(out=x_table[g][:].bitcast(I32), in_=x_words[g].rearrange("p n t -> p (n t)").bitcast(I32))
 
-        def load_weight(name, w, t):
-            for g in range(PASSES):
-                rows = w[g * P * PACK : (g + 1) * P * PACK, t * P : (t + 1) * P]
-                nc.sync.dma_start(out=raw[name, t][:, g, :, :], in_=rows.rearrange("(p j) c -> p j c", j=PACK))
+        def load_weight(name, t):
+            n, s0 = place[name, t]
+            for g in range(source[name].shape[0] // SLAB):
+                rows = source[name][g * SLAB : (g + 1) * SLAB, t * P : (t + 1) * P]
+                nc.sync.dma_start(
+                    out=raw[n][:, s0 + g, :].rearrange("p (j c) -> p j c", j=PACK), in_=rows.rearrange("(p j) c -> p j c", j=PACK)
+                )
 
-        def load_edges(t):
+        def load_a(t):
             nc.sync.dma_start(out=vwa_sb[t][:], in_=vwa[t * P : (t + 1) * P, :])
+
+        def load_b(t):
             nc.sync.dma_start(out=vwb_sb[t][:], in_=vwb[t * P : (t + 1) * P, :])
 
         def load_scales():
@@ -74,8 +100,7 @@ def tile_picked_ytcoda_infl_p_kernel(tc, x_words, x_scales, w1, w2, vwa, vwb, un
                 )
 
         def load_unit():
-            with nc.allow_non_contiguous_dma(reason="one value a partition"):
-                nc.sync.dma_start(out=unit_sb[:], in_=unit.rearrange("(t p) o -> p (t o)", p=P))
+            nc.sync.dma_start(out=unit_rows[0:TILES, :], in_=unit.rearrange("(t p) o -> t (p o)", p=P))
 
         def load_list(tile, src):
             nc.sync.dma_start(tile[:], src)
@@ -83,69 +108,65 @@ def tile_picked_ytcoda_infl_p_kernel(tc, x_words, x_scales, w1, w2, vwa, vwb, un
         load_list(offs_sb, offs)
         load_scales()
         load_words(0)
-        load_weight("w1", w1, 0)
+        load_weight("w1", 0)
         load_words(1)
-        load_weight("w2", w2, 0)
         load_list(up1_sb, up1)
-        load_edges(0)
         load_list(up2_sb, up2)
+        load_weight("w1", 1)
+        load_a(0)
         load_unit()
-        load_weight("w1", w1, 1)
-        load_weight("w2", w2, 1)
-        load_edges(1)
-        load_weight("w1", w1, 2)
-        load_weight("w2", w2, 2)
-        load_edges(2)
-        load_weight("w1", w1, 3)
-        load_weight("w2", w2, 3)
-        load_edges(3)
-        nc.sync.dma_start(out=w3_raw[:], in_=w3.rearrange("(p j) c -> p j c", j=PACK))
+        load_weight("w2", 0)
+        load_b(0)
+        load_weight("w1", 2)
+        load_weight("w2", 1)
+        load_a(1)
+        load_b(1)
+        load_weight("w1", 3)
+        load_weight("w2", 2)
+        load_a(2)
+        load_b(2)
+        load_weight("w2", 3)
+        load_weight("w3", 0)
+        load_a(3)
+        load_b(3)
 
-        warm = keep.tile([P, 2], F32, name="warm")
-        nc.gpsimd.memset(warm[:, 0:1], 1.0)
-        nc.scalar.activation(warm[:, 1:2], warm[:, 0:1], ACT.Abs_reciprocal_sqrt)
         make_identity(nc, ident[:])
         for t in range(TILES):
             nc.gpsimd.memset(act[t][:, S:], 0.0)
             nc.gpsimd.memset(score[t][:, S:], 0.0)
 
+        state = {}
+        V = nc.vector.tensor_copy
+        A = nc.scalar.copy
+
+        def turn_unit():
+            turned = psum.tile([P, P], F32, name="back", bufs=2)
+            nc.tensor.transpose(turned[:], unit_rows[:], ident[:])
+            nc.scalar.copy(unit_sb[:], turned[:, 0:TILES])
+
         def pick(dst, table):
             nc.vector.tensor_copy(dst[:], table[:].indirect(offs_sb[:]))
 
-        def quantise(name, t, copy):
-            if (name, t) in host:
-                grouped = host[name, t].bitcast(BF16).rearrange("p (g c j) -> p g c j", g=PASSES, j=PACK)
-            else:
-                grouped = ring.tile([P, PASSES, P, PACK], BF16, name="grouped", align_bytes=64, bufs=4)
-            copy(
-                grouped[:].rearrange("p g (c i) j -> p g c j i", i=4),
-                raw[name, t][:].rearrange("p g j (c i) -> p g c j i", i=4),
-            )
-            codes = keep.tile([P, PASSES * P], U32, name="codes_%s_%d" % (name, t), align_bytes=64)
-            planes = keep.tile([P, PASSES * P], U8, name="planes_%s_%d" % (name, t), align_bytes=64)
-            nc.vector.quantize_mx(out=codes[:].bitcast(FP8X4), scales=planes[:], in_=grouped[:].rearrange("p g c j -> p (g c j)"))
-            quantised[name, t] = (codes, planes)
-
-        def quantise_by_pass(name, t, copy):
-            codes = keep.tile([P, PASSES * P], U32, name="codes_%s_%d" % (name, t), align_bytes=64)
-            planes = keep.tile([P, PASSES * P], U8, name="planes_%s_%d" % (name, t), align_bytes=64)
-            grouped = ring.tile([P, PASSES, P, PACK], BF16, name="grouped", align_bytes=64, bufs=4)
-            for g in range(PASSES):
+        def quantise(n, copy, pieces=1):
+            slabs = raw[n].shape[1]
+            grouped = keep.tile([P, slabs, SLAB], BF16, name="grouped%d" % n, align_bytes=64)
+            step = slabs // pieces
+            for s0 in range(0, slabs, step):
                 copy(
-                    grouped[:, g, :, :].rearrange("p (c i) j -> p c j i", i=4),
-                    raw[name, t][:, g, :, :].rearrange("p j (c i) -> p c j i", i=4),
+                    grouped[:, s0 : s0 + step, :].rearrange("p g (c i j) -> p g c j i", i=4, j=PACK),
+                    raw[n][:, s0 : s0 + step, :].rearrange("p g (j c i) -> p g c j i", i=4, j=PACK),
                 )
-            nc.vector.quantize_mx(out=codes[:].bitcast(FP8X4), scales=planes[:], in_=grouped[:].rearrange("p g c j -> p (g c j)"))
-            quantised[name, t] = (codes, planes)
+            nc.vector.quantize_mx(out=codes[n][:].bitcast(FP8X4), scales=planes[n][:], in_=grouped[:].rearrange("p g e -> p (g e)"))
 
         def product(name, t):
-            codes, planes = quantised[name, t]
+            n, s0 = place[name, t]
             acc = psum.tile([P, S], F32, name="acc_" + name)
             for g in range(PASSES):
+                cols = slice((s0 + g) * P, (s0 + g + 1) * P)
                 nc.tensor.matmul_mx(
                     out=acc[:],
-                    lhsT=codes[:, g * P : (g + 1) * P].bitcast(FP8X4),
-                    lhsT_scale=planes[:, g * P : (g + 1) * P],
+                    lhsT=codes[n][:, cols].bitcast(FP8X4),
+                    lhsT_scale=planes[n][:, cols],
                     rhs=x_codes[g][:].bitcast(FP8X4),
                     rhs_scale=x_planes[4 * g :, :],
                     start=(g == 0),
@@ -161,79 +182,75 @@ def tile_picked_ytcoda_infl_p_kernel(tc, x_words, x_scales, w1, w2, vwa, vwb, un
             acc = product("w2", t)
             nc.scalar.activation(score[t][:, :S], acc[:], ACT.Copy, scale=unit_sb[:, t : t + 1])
 
-        def add_turned(bank, a, b, blocks):
+        def add_turned(bank, parts, blocks):
             for jb in range(blocks):
                 cols = slice(jb * P, (jb + 1) * P)
-                nc.tensor.matmul(bank[:, jb, :], lhsT=a[:, cols], rhs=ident[:], start=True, stop=False, is_transpose=True)
-                nc.tensor.matmul(bank[:, jb, :], lhsT=b[:, cols], rhs=ident[:], start=False, stop=True, is_transpose=True)
+                for k, part in enumerate(parts):
+                    nc.tensor.matmul(
+                        bank[:, jb, :], lhsT=part[:, cols], rhs=ident[:], start=(k == 0), stop=(k == len(parts) - 1), is_transpose=True
+                    )
 
         def fetch(name, table, order, t, b0, b1):
-            got = keep.tile([P, (b1 - b0) * P], F32, name="%s_%d_%d" % (name, t, b0))
-            nc.scalar.activation(got[:], table[t][:].indirect(order[:, 8 * b0 : 8 * b1]), ACT.Copy)
-            state[t, b0, name] = got
+            if (t, name) not in state:
+                state[t, name] = keep.tile([P, S], F32, name="%s_%d" % (name, t))
+            nc.scalar.activation(state[t, name][:, b0 * P : b1 * P], table[t][:].indirect(order[:, 8 * b0 : 8 * b1]), ACT.Copy)
+            for b in range(b0, b1):
+                state[t, b, name] = True
 
-        def fetch2(t, b0, b1):
-            fetch("a2", act, up2_sb, t, b0, b1)
-
-        def fetch1(t, b0, b1):
+        def fetch1(t, b0=0, b1=JB):
             fetch("a1", act, up1_sb, t, b0, b1)
 
-        def fetch3(t, b0, b1):
+        def fetch2(t, b0=0, b1=JB):
+            fetch("a2", act, up2_sb, t, b0, b1)
+
+        def fetch3(t, b0=0, b1=JB):
             fetch("w1s", score, up1_sb, t, b0, b1)
 
         def looked(name, table, order, t, b0, b1):
             if (t, b0, name) in state:
-                return state[t, b0, name][:]
+                return state[t, name][:, b0 * P : b1 * P]
             return table[t][:].indirect(order[:, 8 * b0 : 8 * b1])
 
-        def edge1(t, b0, b1):
-            edge = edge_tiles[t][:, :, b0 * P : b1 * P]
-            nc.vector.tensor_tensor(edge[:, 0, :], looked("a1", act, up1_sb, t, b0, b1), vwa_sb[t][:, b0 * P : b1 * P], ALU.mult)
-            state[t, b0, "edge"] = edge
+        def edge1(t, b0=0, b1=JB):
+            nc.vector.tensor_tensor(edge[t][:, 0, b0 * P : b1 * P], looked("a1", act, up1_sb, t, b0, b1), vwa_sb[t][:, b0 * P : b1 * P], ALU.mult)
 
-        def edge2(t, b0, b1):
-            edge = edge_tiles[t][:, :, b0 * P : b1 * P]
-            nc.vector.tensor_tensor(edge[:, 1, :], looked("a2", act, up2_sb, t, b0, b1), vwb_sb[t][:, b0 * P : b1 * P], ALU.mult)
+        def edge2(t, b0=0, b1=JB):
+            nc.vector.tensor_tensor(edge[t][:, 1, b0 * P : b1 * P], looked("a2", act, up2_sb, t, b0, b1), vwb_sb[t][:, b0 * P : b1 * P], ALU.mult)
 
-        def edges(t, b0, b1):
-            edge1(t, b0, b1)
-            edge2(t, b0, b1)
-
-        def sizes(t, b0, b1):
-            n = (b1 - b0) * P
-            size = ring.tile([P, 2, n], F32, name="size", bufs=3)
-            nc.scalar.activation(size[:], state[t, b0, "edge"][:], ACT.Abs)
+        def sizes(t, b0=0, b1=JB):
+            size = ring.tile([P, 2, (b1 - b0) * P], F32, name="size", bufs=2)
+            nc.scalar.activation(size[:], edge[t][:, :, b0 * P : b1 * P], ACT.Abs)
             tot = psum.tile([P, b1 - b0, P], F32, name="tot", bufs=2)
-            add_turned(tot, size[:, 0, :], size[:, 1, :], b1 - b0)
+            add_turned(tot, [size[:, 0, :], size[:, 1, :]], b1 - b0)
             state[t, b0, "tot"] = tot
 
-        def invert(t, b0, b1):
-            n = (b1 - b0) * P
-            square = ring.tile([P, n], F32, name="square")
-            nc.scalar.activation(square[:], state[t, b0, "tot"][:].rearrange("p b i -> p (b i)"), ACT.Square, bias=SHIFT)
-            inverse = ring.tile([P, b1 - b0, P], F32, name="inverse", bufs=3)
-            nc.scalar.activation(inverse[:].rearrange("p b i -> p (b i)"), square[:], ACT.Abs_reciprocal_sqrt)
-            state[t, b0, "inverse"] = inverse
+        def sizes_v(t, b0=0, b1=JB):
+            size = ring.tile([P, 2, (b1 - b0) * P], F32, name="size", bufs=2)
+            part = edge[t][:, :, b0 * P : b1 * P]
+            nc.vector.tensor_scalar(size[:], part, -2.0, 0.0, ALU.mult, ALU.max)
+            tot = psum.tile([P, b1 - b0, P], F32, name="tot", bufs=2)
+            add_turned(tot, [size[:, 0, :], part[:, 0, :], size[:, 1, :], part[:, 1, :]], b1 - b0)
+            state[t, b0, "tot"] = tot
 
-        def carried(t, b0, b1):
-            n = (b1 - b0) * P
-            edge = state[t, b0, "edge"]
-            term = terms[t][:, :, b0 * P : b1 * P]
-            nc.vector.tensor_tensor(term[:, 1, :], score[t][:, b0 * P : b1 * P], edge[:, 1, :], ALU.mult)
-            nc.vector.tensor_tensor(term[:, 0, :], looked("w1s", score, up1_sb, t, b0, b1), edge[:, 0, :], ALU.mult)
-            num = psum.tile([P, b1 - b0, P], F32, name="num", bufs=2)
-            add_turned(num, term[:, 0, :], term[:, 1, :], b1 - b0)
+        def invert(t, b0=0, b1=JB):
+            square = ring.tile([P, (b1 - b0) * P], F32, name="square")
+            nc.scalar.activation(square[:], state[t, b0, "tot"][:].rearrange("p b i -> p (b i)"), ACT.Square, bias=SHIFT)
+            if (t, "inverse") not in state:
+                state[t, "inverse"] = keep.tile([P, JB, P], F32, name="inverse%d" % t)
+            nc.scalar.activation(state[t, "inverse"][:, b0:b1, :].rearrange("p b i -> p (b i)"), square[:], ACT.Abs_reciprocal_sqrt)
+
+        def own(t, b0=0, b1=JB):
+            nc.vector.tensor_tensor(term[t][:, 1, b0 * P : b1 * P], score[t][:, b0 * P : b1 * P], edge[t][:, 1, b0 * P : b1 * P], ALU.mult)
+
+        def first(t, b0=0, b1=JB, bank="num"):
+            part = term[t][:, :, b0 * P : b1 * P]
+            nc.vector.tensor_tensor(part[:, 0, :], looked("w1s", score, up1_sb, t, b0, b1), edge[t][:, 0, b0 * P : b1 * P], ALU.mult)
+            num = psum.tile([P, b1 - b0, P], F32, name=bank, bufs=BUFS[bank])
+            add_turned(num, [part[:, 0, :], part[:, 1, :]], b1 - b0)
             state[t, b0, "num"] = num
 
-        def finish(t, b0, b1):
-            nc.vector.tensor_tensor(hid_t[:, b0:b1, t * P : (t + 1) * P], state[t, b0, "num"][:], state[t, b0, "inverse"][:], ALU.mult)
-
-        def quantise_w3():
-            w3_grouped = keep.tile([P, N, PACK], BF16, name="w3_grouped", align_bytes=64)
-            nc.vector.tensor_copy(
-                w3_grouped[:].rearrange("p (c i) j -> p c j i", i=4), w3_raw[:].rearrange("p j (c i) -> p c j i", i=4)
-            )
-            nc.vector.quantize_mx(out=w3_codes[:].bitcast(FP8X4), scales=w3_planes[:], in_=w3_grouped[:].rearrange("p c j -> p (c j)"))
+        def finish(t, b0=0, b1=JB):
+            nc.vector.tensor_tensor(hid_t[:, b0:b1, t * P : (t + 1) * P], state[t, b0, "num"][:], state[t, "inverse"][:, b0:b1, :], ALU.mult)
 
         def logits(b0, b1, copy, acc_name, evac):
             nb = b1 - b0
@@ -249,11 +266,12 @@ def tile_picked_ytcoda_infl_p_kernel(tc, x_words, x_scales, w1, w2, vwa, vwb, un
             hid_codes = keep.tile([P, n], U32, name="hid_codes%d" % b0, align_bytes=64)
             hid_planes = keep.tile([P, n], U8, name="hid_planes%d" % b0, align_bytes=64)
             nc.vector.quantize_mx(out=hid_codes[:].bitcast(FP8X4), scales=hid_planes[:], in_=hid_grouped[:].rearrange("p c j -> p (c j)"))
-            acc = psum.tile([P, S], F32, name=acc_name)
+            g3, s3 = place["w3", 0]
+            acc = psum.tile([P, S], F32, name=acc_name, bufs=BUFS[acc_name])
             nc.tensor.matmul_mx(
                 out=acc[:, :n],
-                lhsT=w3_codes[:].bitcast(FP8X4),
-                lhsT_scale=w3_planes[:],
+                lhsT=codes[g3][:, s3 * P : (s3 + 1) * P].bitcast(FP8X4),
+                lhsT_scale=planes[g3][:, s3 * P : (s3 + 1) * P],
                 rhs=hid_codes[:].bitcast(FP8X4),
                 rhs_scale=hid_planes[:],
                 start=True,
@@ -263,75 +281,67 @@ def tile_picked_ytcoda_infl_p_kernel(tc, x_words, x_scales, w1, w2, vwa, vwb, un
             evac(result[:], acc[:, :n])
             nc.sync.dma_start(out=out[:, b0 * P : b1 * P], in_=result[:])
 
-        w3_codes = keep.tile([P, N], U32, name="w3_codes", align_bytes=64)
-        w3_planes = keep.tile([P, N], U8, name="w3_planes", align_bytes=64)
-        terms = [keep.tile([P, 2, S], F32, name="term%d" % t, align_bytes=64) for t in range(TILES)]
-        edge_tiles = [keep.tile([P, 2, S], F32, name="edge%d" % t, align_bytes=64) for t in range(TILES)]
-        host = { }
-        quantised = {}
-        state = {}
-        V = nc.vector.tensor_copy
-        A = nc.scalar.copy
         pick(x_planes, scale_table)
         pick(x_codes[0], x_table[0])
-        quantise_by_pass("w1",0,A)
+        quantise(0, A, 2)
         pick(x_codes[1], x_table[1])
         make_act(0)
-        quantise("w2",0,V)
-        make_score(0)
-        edge1(0,0,4)
-        fetch2(0,0,4)
-        fetch3(0,0,4)
-        quantise("w1",1,V)
+        turn_unit()
+        quantise(1, V)
+        fetch2(0)
         make_act(1)
-        edge2(0,0,4)
-        quantise("w2",1,V)
-        make_score(1)
-        carried(0,0,4)
-        sizes(0,0,4)
-        edge1(1,0,4)
-        fetch2(1,0,4)
-        fetch3(1,0,4)
-        quantise("w1",2,V)
+        edge1(0)
+        quantise(2, V)
+        edge2(0)
+        make_score(0)
+        sizes(0)
+        quantise(3, V)
+        fetch2(1)
         make_act(2)
-        edge2(1,0,4)
-        invert(0,0,4)
-        quantise("w2",2,V)
-        make_score(2)
-        carried(1,0,4)
-        sizes(1,0,4)
-        finish(0,0,4)
-        edge1(2,0,4)
-        fetch2(2,0,4)
-        fetch3(2,0,4)
-        quantise("w1",3,V)
+        fetch3(0)
+        edge1(1)
+        invert(0)
+        edge2(1)
+        make_score(1)
+        own(0)
+        first(0)
+        sizes(1)
+        finish(0)
+        quantise(4, V)
+        fetch2(2)
         make_act(3)
-        edge2(2,0,4)
-        invert(1,0,4)
-        quantise("w2",3,V)
+        fetch3(1)
+        edge1(2)
+        invert(1)
+        edge2(2)
+        make_score(2)
+        own(1)
+        first(1)
+        sizes(2)
+        finish(1)
+        quantise(5, V)
+        fetch3(2)
+        edge1(3)
+        invert(2)
+        own(2)
+        first(2)
+        edge2(3)
         make_score(3)
-        carried(2,0,4)
-        sizes(2,0,4)
-        finish(1,0,4)
-        edges(3,0,2)
-        invert(2,0,4)
-        quantise_w3()
         sizes(3,0,2)
-        fetch3(3,0,2)
-        edges(3,2,3)
-        carried(3,0,2)
+        sizes(3,2,4)
+        finish(2)
         invert(3,0,2)
-        sizes(3,2,3)
-        edges(3,3,4)
-        finish(2,0,4)
-        finish(3,0,2)
-        invert(3,2,3)
-        carried(3,2,3)
-        sizes(3,3,4)
-        logits(0,2,A,"acc_w1",A)
-        carried(3,3,4)
-        invert(3,3,4)
+        invert(3,2,4)
+        own(3)
+        first(3,0,1,"acc_w1")
+        first(3,1,2,"acc_w2")
+        finish(3,0,1)
+        first(3,2,3)
+        finish(3,1,2)
+        logits(0,1,A,"tot",A)
+        first(3,3,4)
+        logits(1,2,A,"tot",A)
         finish(3,2,3)
         finish(3,3,4)
-        logits(2,3,A,"acc_w2",A)
-        logits(3,4,A,"acc_w1",A)
+        logits(2,3,A,"tot",A)
+        logits(3,4,A,"tot",A)

@@ -14,33 +14,46 @@ U16 = mybir.dt.uint16
 U8 = mybir.dt.uint8
 FP8X4 = mybir.dt.float8_e4m3fn_x4
 ACT = mybir.ActivationFunctionType
-ALU = mybir.AluOpType
+MULT = mybir.AluOpType.mult
 
 P = 128
 PACK = 4
-PASSES = K // (P * PACK)
+SLAB = PACK * P
+PASSES = K // SLAB
 TILES = H // P
-JB = S // P
+LAST = TILES - 1
+BLOCKS = S // P
+LIST_COLS = P // 16
 PAD = 32
 SHIFT = 0.2
-SLAB = PACK * P
-BUFS = {"num": 2, "tot": 2, "back": 2, "acc_w1": 1, "acc_w2": 1}
+PSUM_BUFS = {"acc_w1": 1, "acc_w2": 1, "tot": 2, "num": 2, "back": 2}
+
+GROUPS = (
+    [[("w1", 0)], [("w1", 1)], [("w2", 0)]]
+    + [[("w1", t + 1), ("w2", t)] for t in range(1, LAST)]
+    + [[("w2", LAST), ("w3", 0)]]
+)
 
 
-def tile_picked_ytcoda_infl_p_kernel(tc, x_words, x_scales, w1, w2, vwa, vwb, unit, w3, offs, up1, up2, out):
+def tile_picked_ytcoda_infl_p_kernel(
+    tc, x_words, x_scales, w1, w2, vwa, vwb, unit, w3, offs, up1, up2, out
+):
     nc = tc.nc
     with ExitStack() as ctx:
         keep = ctx.enter_context(tc.tile_pool(name="keep", bufs=1))
         ring = ctx.enter_context(tc.tile_pool(name="ring", bufs=2))
         psum = ctx.enter_context(tc.psum_pool(name="psum", bufs=1))
 
+        def bank(tag, shape):
+            return psum.tile(shape, F32, name=tag, bufs=PSUM_BUFS[tag])
+
         offs_sb = keep.tile([P, S // 16], U16, name="offs_sb")
         up1_sb = keep.tile([P, S // 16], U16, name="up1_sb")
         up2_sb = keep.tile([P, S // 16], U16, name="up2_sb")
-        x_table = [keep.tile([P, T], U32, name="x_table%d" % g, align_bytes=64) for g in range(PASSES)]
+        word_table = [keep.tile([P, T], U32, name="word_table%d" % g, align_bytes=64) for g in range(PASSES)]
         scale_table = keep.tile([P, T], U8, name="scale_table", align_bytes=64)
         x_codes = [keep.tile([P, S], U32, name="x_codes%d" % g, align_bytes=64) for g in range(PASSES)]
-        x_planes = keep.tile([P, S], U8, name="x_planes", align_bytes=64)
+        x_bytes = keep.tile([P, S], U8, name="x_bytes", align_bytes=64)
         ident = keep.tile([P, P], F32, name="ident")
         unit_rows = keep.tile([P, P], F32, name="unit_rows")
         unit_sb = keep.tile([P, TILES], F32, name="unit_sb")
@@ -48,26 +61,25 @@ def tile_picked_ytcoda_infl_p_kernel(tc, x_words, x_scales, w1, w2, vwa, vwb, un
         vwb_sb = [keep.tile([P, S], F32, name="vwb%d" % t) for t in range(TILES)]
         act = [keep.tile([P, S + PAD], F32, name="act%d" % t) for t in range(TILES)]
         score = [keep.tile([P, S + PAD], F32, name="score%d" % t) for t in range(TILES)]
-        hid_t = keep.tile([P, JB, H], BF16, name="hid_t", align_bytes=64)
+        hid_turned = keep.tile([P, BLOCKS, H], BF16, name="hid_turned", align_bytes=64)
 
-        groups = [[("w1", 0)], [("w1", 1)], [("w2", 0)], [("w1", 2), ("w2", 1)], [("w1", 3), ("w2", 2)], [("w2", 3), ("w3", 0)]]
-        source = {"w1": w1, "w2": w2, "w3": w3}
-        raw, codes, planes, place = [], [], [], {}
-        for n, group in enumerate(groups):
+        weights = {"w1": w1, "w2": w2, "w3": w3}
+        raw, w_codes, w_bytes, place = [], [], [], {}
+        for n, group in enumerate(GROUPS):
             slabs = 0
             for name, t in group:
                 place[name, t] = (n, slabs)
-                slabs = slabs + source[name].shape[0] // SLAB
+                slabs = slabs + weights[name].shape[0] // SLAB
             raw.append(keep.tile([P, slabs, SLAB], F32, name="raw_%d" % n, align_bytes=64))
-            codes.append(keep.tile([P, slabs * P], U32, name="codes%d" % n, align_bytes=64))
-            planes.append(keep.tile([P, slabs * P], U8, name="planes%d" % n, align_bytes=64))
+            w_codes.append(keep.tile([P, slabs * P], U32, name="w_codes%d" % n, align_bytes=64))
+            w_bytes.append(keep.tile([P, slabs * P], U8, name="w_bytes%d" % n, align_bytes=64))
 
-        def home(name, t):
+        def spent(name, t):
             n, s0 = place[name, t]
             return raw[n][:, s0 : s0 + PASSES, :]
 
-        edge = [home("w1", 1), home("w1", 2), home("w1", 3), home("w2", 3)]
-        term = [home("w2", 1), home("w2", 2), home("w1", 0), home("w2", 0)]
+        edge = [spent("w1", t + 1) for t in range(LAST)] + [spent("w2", LAST)]
+        term = [spent("w2", 1), spent("w2", 2), spent("w1", 0), spent("w2", 0)]
 
         nc.gpsimd.memset(scale_table[:].bitcast(I32), 0)
         nc.gpsimd.memset(unit_rows[:], 0.0)
@@ -76,73 +88,48 @@ def tile_picked_ytcoda_infl_p_kernel(tc, x_words, x_scales, w1, w2, vwa, vwb, un
         nc.scalar.activation(warm[:, 1:2], warm[:, 0:1], ACT.Abs_reciprocal_sqrt)
 
         def load_words(g):
-            nc.sync.dma_start(out=x_table[g][:].bitcast(I32), in_=x_words[g].rearrange("p n t -> p (n t)").bitcast(I32))
-
-        def load_weight(name, t):
-            n, s0 = place[name, t]
-            for g in range(source[name].shape[0] // SLAB):
-                rows = source[name][g * SLAB : (g + 1) * SLAB, t * P : (t + 1) * P]
-                nc.sync.dma_start(
-                    out=raw[n][:, s0 + g, :].rearrange("p (j c) -> p j c", j=PACK), in_=rows.rearrange("(p j) c -> p j c", j=PACK)
-                )
-
-        def load_a(t):
-            nc.sync.dma_start(out=vwa_sb[t][:], in_=vwa[t * P : (t + 1) * P, :])
-
-        def load_b(t):
-            nc.sync.dma_start(out=vwb_sb[t][:], in_=vwb[t * P : (t + 1) * P, :])
+            words = x_words[g].rearrange("p n r -> p (n r)").bitcast(I32)
+            nc.sync.dma_start(out=word_table[g][:].bitcast(I32), in_=words)
 
         def load_scales():
             for q in range(4):
+                rows = x_scales[:, 4 * q : 4 * q + 4, :].bitcast(I32)
+                nc.sync.dma_start(out=scale_table[32 * q : 32 * q + 4 * PASSES, :].bitcast(I32), in_=rows)
+
+        def load_weight(name, t):
+            n, s0 = place[name, t]
+            for g in range(weights[name].shape[0] // SLAB):
+                rows = weights[name][g * SLAB : (g + 1) * SLAB, t * P : (t + 1) * P]
                 nc.sync.dma_start(
-                    out=scale_table[32 * q : 32 * q + 4 * PASSES, :].bitcast(I32),
-                    in_=x_scales[:, 4 * q : 4 * q + 4, :].bitcast(I32),
+                    out=raw[n][:, s0 + g, :].rearrange("p (r c) -> p r c", r=PACK),
+                    in_=rows.rearrange("(p r) c -> p r c", r=PACK),
                 )
 
-        def load_unit():
-            nc.sync.dma_start(out=unit_rows[0:TILES, :], in_=unit.rearrange("(t p) o -> t (p o)", p=P))
+        def load_rows(dst, src, t):
+            nc.sync.dma_start(out=dst[t][:], in_=src[t * P : (t + 1) * P, :])
 
-        def load_list(tile, src):
-            nc.sync.dma_start(tile[:], src)
-
-        load_list(offs_sb, offs)
-        load_scales()
+        nc.sync.dma_start(offs_sb[:], offs)
         load_words(0)
+        load_scales()
         load_weight("w1", 0)
         load_words(1)
-        load_list(up1_sb, up1)
-        load_list(up2_sb, up2)
+        nc.sync.dma_start(up1_sb[:], up1)
+        nc.sync.dma_start(up2_sb[:], up2)
         load_weight("w1", 1)
-        load_a(0)
-        load_unit()
+        load_rows(vwa_sb, vwa, 0)
+        nc.sync.dma_start(out=unit_rows[0:TILES, :], in_=unit.rearrange("(t p) o -> t (p o)", p=P))
         load_weight("w2", 0)
-        load_b(0)
-        load_weight("w1", 2)
-        load_weight("w2", 1)
-        load_a(1)
-        load_b(1)
-        load_weight("w1", 3)
-        load_weight("w2", 2)
-        load_a(2)
-        load_b(2)
-        load_weight("w2", 3)
-        load_weight("w3", 0)
-        load_a(3)
-        load_b(3)
+        load_rows(vwb_sb, vwb, 0)
+        for t in range(1, TILES):
+            for name, tile in GROUPS[t + 2]:
+                load_weight(name, tile)
+            load_rows(vwa_sb, vwa, t)
+            load_rows(vwb_sb, vwb, t)
 
         make_identity(nc, ident[:])
         for t in range(TILES):
             nc.gpsimd.memset(act[t][:, S:], 0.0)
             nc.gpsimd.memset(score[t][:, S:], 0.0)
-
-        state = {}
-        V = nc.vector.tensor_copy
-        A = nc.scalar.copy
-
-        def turn_unit():
-            turned = psum.tile([P, P], F32, name="back", bufs=2)
-            nc.tensor.transpose(turned[:], unit_rows[:], ident[:])
-            nc.scalar.copy(unit_sb[:], turned[:, 0:TILES])
 
         def pick(dst, table):
             nc.vector.tensor_copy(dst[:], table[:].indirect(offs_sb[:]))
@@ -153,195 +140,171 @@ def tile_picked_ytcoda_infl_p_kernel(tc, x_words, x_scales, w1, w2, vwa, vwb, un
             step = slabs // pieces
             for s0 in range(0, slabs, step):
                 copy(
-                    grouped[:, s0 : s0 + step, :].rearrange("p g (c i j) -> p g c j i", i=4, j=PACK),
-                    raw[n][:, s0 : s0 + step, :].rearrange("p g (j c i) -> p g c j i", i=4, j=PACK),
+                    grouped[:, s0 : s0 + step, :].rearrange("p s (c i r) -> p s c r i", i=4, r=PACK),
+                    raw[n][:, s0 : s0 + step, :].rearrange("p s (r c i) -> p s c r i", i=4, r=PACK),
                 )
-            nc.vector.quantize_mx(out=codes[n][:].bitcast(FP8X4), scales=planes[n][:], in_=grouped[:].rearrange("p g e -> p (g e)"))
+            nc.vector.quantize_mx(
+                out=w_codes[n][:].bitcast(FP8X4), scales=w_bytes[n][:], in_=grouped[:].rearrange("p s e -> p (s e)")
+            )
+
+        def stationary(name, t, g):
+            n, s0 = place[name, t]
+            cols = slice((s0 + g) * P, (s0 + g + 1) * P)
+            return {"lhsT": w_codes[n][:, cols].bitcast(FP8X4), "lhsT_scale": w_bytes[n][:, cols]}
 
         def product(name, t):
-            n, s0 = place[name, t]
-            acc = psum.tile([P, S], F32, name="acc_" + name)
+            acc = bank("acc_" + name, [P, S])
             for g in range(PASSES):
-                cols = slice((s0 + g) * P, (s0 + g + 1) * P)
                 nc.tensor.matmul_mx(
                     out=acc[:],
-                    lhsT=codes[n][:, cols].bitcast(FP8X4),
-                    lhsT_scale=planes[n][:, cols],
                     rhs=x_codes[g][:].bitcast(FP8X4),
-                    rhs_scale=x_planes[4 * g :, :],
+                    rhs_scale=x_bytes[4 * g :, :],
                     start=(g == 0),
                     stop=(g == PASSES - 1),
+                    **stationary(name, t, g),
                 )
             return acc
 
         def make_act(t):
-            acc = product("w1", t)
-            nc.scalar.activation(act[t][:, :S], acc[:], ACT.Relu, bias=-SHIFT)
+            nc.scalar.activation(act[t][:, :S], product("w1", t)[:], ACT.Relu, bias=-SHIFT)
 
         def make_score(t):
-            acc = product("w2", t)
-            nc.scalar.activation(score[t][:, :S], acc[:], ACT.Copy, scale=unit_sb[:, t : t + 1])
+            nc.scalar.activation(score[t][:, :S], product("w2", t)[:], ACT.Copy, scale=unit_sb[:, t : t + 1])
 
-        def add_turned(bank, parts, blocks):
-            for jb in range(blocks):
-                cols = slice(jb * P, (jb + 1) * P)
-                for k, part in enumerate(parts):
+        def turn_unit():
+            turned = bank("back", [P, P])
+            nc.tensor.transpose(turned[:], unit_rows[:], ident[:])
+            nc.scalar.copy(unit_sb[:], turned[:, 0:TILES])
+
+        def fetch(window, order, name):
+            fetched = keep.tile([P, S], F32, name=name)
+            nc.scalar.activation(fetched[:], window[:].indirect(order[:]), ACT.Copy)
+            return fetched[:]
+
+        def add_turned(tag, pair, blocks):
+            total = bank(tag, [P, blocks, P])
+            for b in range(blocks):
+                for e in range(2):
                     nc.tensor.matmul(
-                        bank[:, jb, :], lhsT=part[:, cols], rhs=ident[:], start=(k == 0), stop=(k == len(parts) - 1), is_transpose=True
+                        total[:, b, :],
+                        lhsT=pair[:, e, b * P : (b + 1) * P],
+                        rhs=ident[:],
+                        start=(e == 0),
+                        stop=(e == 1),
+                        is_transpose=True,
                     )
+            return total
 
-        def fetch(name, table, order, t, b0, b1):
-            if (t, name) not in state:
-                state[t, name] = keep.tile([P, S], F32, name="%s_%d" % (name, t))
-            nc.scalar.activation(state[t, name][:, b0 * P : b1 * P], table[t][:].indirect(order[:, 8 * b0 : 8 * b1]), ACT.Copy)
-            for b in range(b0, b1):
-                state[t, b, name] = True
+        def make_edge1(t):
+            nc.vector.tensor_tensor(edge[t][:, 0, :], act[t][:].indirect(up1_sb[:]), vwa_sb[t][:], MULT)
 
-        def fetch1(t, b0=0, b1=JB):
-            fetch("a1", act, up1_sb, t, b0, b1)
+        def make_edge2(t, act_up2):
+            nc.vector.tensor_tensor(edge[t][:, 1, :], act_up2, vwb_sb[t][:], MULT)
 
-        def fetch2(t, b0=0, b1=JB):
-            fetch("a2", act, up2_sb, t, b0, b1)
+        def sum_sizes(t, b0, b1):
+            sizes = ring.tile([P, 2, (b1 - b0) * P], F32, name="sizes")
+            nc.scalar.activation(sizes[:], edge[t][:, :, b0 * P : b1 * P], ACT.Abs)
+            return add_turned("tot", sizes, b1 - b0)
 
-        def fetch3(t, b0=0, b1=JB):
-            fetch("w1s", score, up1_sb, t, b0, b1)
+        def invert(inverse, size_sum):
+            square = ring.tile([P, size_sum.shape[1] * P], F32, name="square")
+            nc.scalar.activation(square[:], size_sum[:].rearrange("p b i -> p (b i)"), ACT.Square, bias=SHIFT)
+            nc.scalar.activation(inverse.rearrange("p b i -> p (b i)"), square[:], ACT.Abs_reciprocal_sqrt)
 
-        def looked(name, table, order, t, b0, b1):
-            if (t, b0, name) in state:
-                return state[t, name][:, b0 * P : b1 * P]
-            return table[t][:].indirect(order[:, 8 * b0 : 8 * b1])
+        def make_term2(t):
+            nc.vector.tensor_tensor(term[t][:, 1, :], score[t][:, :S], edge[t][:, 1, :], MULT)
 
-        def edge1(t, b0=0, b1=JB):
-            nc.vector.tensor_tensor(edge[t][:, 0, b0 * P : b1 * P], looked("a1", act, up1_sb, t, b0, b1), vwa_sb[t][:, b0 * P : b1 * P], ALU.mult)
+        def sum_terms(t, score_up1, b0, b1, tag):
+            cols = slice(b0 * P, b1 * P)
+            nc.vector.tensor_tensor(term[t][:, 0, cols], score_up1, edge[t][:, 0, cols], MULT)
+            return add_turned(tag, term[t][:, :, cols], b1 - b0)
 
-        def edge2(t, b0=0, b1=JB):
-            nc.vector.tensor_tensor(edge[t][:, 1, b0 * P : b1 * P], looked("a2", act, up2_sb, t, b0, b1), vwb_sb[t][:, b0 * P : b1 * P], ALU.mult)
+        def make_hid(t, b0, b1, term_sum, inverse):
+            nc.vector.tensor_tensor(hid_turned[:, b0:b1, t * P : (t + 1) * P], term_sum[:], inverse[:, b0:b1, :], MULT)
 
-        def sizes(t, b0=0, b1=JB):
-            size = ring.tile([P, 2, (b1 - b0) * P], F32, name="size", bufs=2)
-            nc.scalar.activation(size[:], edge[t][:, :, b0 * P : b1 * P], ACT.Abs)
-            tot = psum.tile([P, b1 - b0, P], F32, name="tot", bufs=2)
-            add_turned(tot, [size[:, 0, :], size[:, 1, :]], b1 - b0)
-            state[t, b0, "tot"] = tot
-
-        def sizes_v(t, b0=0, b1=JB):
-            size = ring.tile([P, 2, (b1 - b0) * P], F32, name="size", bufs=2)
-            part = edge[t][:, :, b0 * P : b1 * P]
-            nc.vector.tensor_scalar(size[:], part, -2.0, 0.0, ALU.mult, ALU.max)
-            tot = psum.tile([P, b1 - b0, P], F32, name="tot", bufs=2)
-            add_turned(tot, [size[:, 0, :], part[:, 0, :], size[:, 1, :], part[:, 1, :]], b1 - b0)
-            state[t, b0, "tot"] = tot
-
-        def invert(t, b0=0, b1=JB):
-            square = ring.tile([P, (b1 - b0) * P], F32, name="square")
-            nc.scalar.activation(square[:], state[t, b0, "tot"][:].rearrange("p b i -> p (b i)"), ACT.Square, bias=SHIFT)
-            if (t, "inverse") not in state:
-                state[t, "inverse"] = keep.tile([P, JB, P], F32, name="inverse%d" % t)
-            nc.scalar.activation(state[t, "inverse"][:, b0:b1, :].rearrange("p b i -> p (b i)"), square[:], ACT.Abs_reciprocal_sqrt)
-
-        def own(t, b0=0, b1=JB):
-            nc.vector.tensor_tensor(term[t][:, 1, b0 * P : b1 * P], score[t][:, b0 * P : b1 * P], edge[t][:, 1, b0 * P : b1 * P], ALU.mult)
-
-        def first(t, b0=0, b1=JB, bank="num"):
-            part = term[t][:, :, b0 * P : b1 * P]
-            nc.vector.tensor_tensor(part[:, 0, :], looked("w1s", score, up1_sb, t, b0, b1), edge[t][:, 0, b0 * P : b1 * P], ALU.mult)
-            num = psum.tile([P, b1 - b0, P], F32, name=bank, bufs=BUFS[bank])
-            add_turned(num, [part[:, 0, :], part[:, 1, :]], b1 - b0)
-            state[t, b0, "num"] = num
-
-        def finish(t, b0=0, b1=JB):
-            nc.vector.tensor_tensor(hid_t[:, b0:b1, t * P : (t + 1) * P], state[t, b0, "num"][:], state[t, "inverse"][:, b0:b1, :], ALU.mult)
-
-        def logits(b0, b1, copy, acc_name, evac):
-            nb = b1 - b0
-            n = nb * P
-            hid_words = hid_t[:].bitcast(F32)
-            back = psum.tile([P, nb, 2, P], F32, name="back", bufs=2)
-            for b in range(nb):
-                for u in range(2):
-                    nc.tensor.transpose(back[:, b, u, :], hid_words[:, b0 + b, u : H // 2 : 2], ident[:])
-            hid_grouped = keep.tile([P, n, PACK], BF16, name="hid_grouped%d" % b0, align_bytes=64)
-            words = hid_grouped[:].bitcast(F32).rearrange("p (b j) u -> p b j u", b=nb)
-            copy(words, back[:].rearrange("p b u j -> p b j u"))
-            hid_codes = keep.tile([P, n], U32, name="hid_codes%d" % b0, align_bytes=64)
-            hid_planes = keep.tile([P, n], U8, name="hid_planes%d" % b0, align_bytes=64)
-            nc.vector.quantize_mx(out=hid_codes[:].bitcast(FP8X4), scales=hid_planes[:], in_=hid_grouped[:].rearrange("p c j -> p (c j)"))
-            g3, s3 = place["w3", 0]
-            acc = psum.tile([P, S], F32, name=acc_name, bufs=BUFS[acc_name])
+        def make_logits(b):
+            pairs = hid_turned[:].bitcast(F32)
+            back = bank("back", [P, 1, 2, P])
+            for u in range(2):
+                nc.tensor.transpose(back[:, 0, u, :], pairs[:, b, u : H // 2 : 2], ident[:])
+            grouped = keep.tile([P, P, PACK], BF16, name="hid_grouped%d" % b, align_bytes=64)
+            nc.scalar.copy(
+                grouped[:].bitcast(F32).rearrange("p (o j) u -> p o j u", o=1), back[:].rearrange("p o u j -> p o j u")
+            )
+            hid_codes = keep.tile([P, P], U32, name="hid_codes%d" % b, align_bytes=64)
+            hid_bytes = keep.tile([P, P], U8, name="hid_bytes%d" % b, align_bytes=64)
+            nc.vector.quantize_mx(
+                out=hid_codes[:].bitcast(FP8X4), scales=hid_bytes[:], in_=grouped[:].rearrange("p j r -> p (j r)")
+            )
+            acc = bank("tot", [P, S])
             nc.tensor.matmul_mx(
-                out=acc[:, :n],
-                lhsT=codes[g3][:, s3 * P : (s3 + 1) * P].bitcast(FP8X4),
-                lhsT_scale=planes[g3][:, s3 * P : (s3 + 1) * P],
+                out=acc[:, :P],
                 rhs=hid_codes[:].bitcast(FP8X4),
-                rhs_scale=hid_planes[:],
+                rhs_scale=hid_bytes[:],
                 start=True,
                 stop=True,
+                **stationary("w3", 0, 0),
             )
-            result = keep.tile([P, n], F32, name="result%d" % b0)
-            evac(result[:], acc[:, :n])
-            nc.sync.dma_start(out=out[:, b0 * P : b1 * P], in_=result[:])
+            result = keep.tile([P, P], F32, name="result%d" % b)
+            nc.scalar.copy(result[:], acc[:, :P])
+            nc.sync.dma_start(out=out[:, b * P : (b + 1) * P], in_=result[:])
 
-        pick(x_planes, scale_table)
-        pick(x_codes[0], x_table[0])
-        quantise(0, A, 2)
-        pick(x_codes[1], x_table[1])
+        pick(x_codes[0], word_table[0])
+        pick(x_bytes, scale_table)
+        quantise(0, nc.scalar.copy, pieces=PASSES)
+        pick(x_codes[1], word_table[1])
         make_act(0)
         turn_unit()
-        quantise(1, V)
-        fetch2(0)
+
+        quantise(1, nc.vector.tensor_copy)
+        act_up2 = fetch(act[0], up2_sb, "act_up2_0")
         make_act(1)
-        edge1(0)
-        quantise(2, V)
-        edge2(0)
+        make_edge1(0)
+        quantise(2, nc.vector.tensor_copy)
+        make_edge2(0, act_up2)
         make_score(0)
-        sizes(0)
-        quantise(3, V)
-        fetch2(1)
-        make_act(2)
-        fetch3(0)
-        edge1(1)
-        invert(0)
-        edge2(1)
-        make_score(1)
-        own(0)
-        first(0)
-        sizes(1)
-        finish(0)
-        quantise(4, V)
-        fetch2(2)
-        make_act(3)
-        fetch3(1)
-        edge1(2)
-        invert(1)
-        edge2(2)
-        make_score(2)
-        own(1)
-        first(1)
-        sizes(2)
-        finish(1)
-        quantise(5, V)
-        fetch3(2)
-        edge1(3)
-        invert(2)
-        own(2)
-        first(2)
-        edge2(3)
-        make_score(3)
-        sizes(3,0,2)
-        sizes(3,2,4)
-        finish(2)
-        invert(3,0,2)
-        invert(3,2,4)
-        own(3)
-        first(3,0,1,"acc_w1")
-        first(3,1,2,"acc_w2")
-        finish(3,0,1)
-        first(3,2,3)
-        finish(3,1,2)
-        logits(0,1,A,"tot",A)
-        first(3,3,4)
-        logits(1,2,A,"tot",A)
-        finish(3,2,3)
-        finish(3,3,4)
-        logits(2,3,A,"tot",A)
-        logits(3,4,A,"tot",A)
+        size_sum = sum_sizes(0, 0, BLOCKS)
+
+        for t in range(1, LAST):
+            quantise(t + 2, nc.vector.tensor_copy)
+            act_up2 = fetch(act[t], up2_sb, "act_up2_%d" % t)
+            make_act(t + 1)
+            score_up1 = fetch(score[t - 1], up1_sb, "score_up1_%d" % (t - 1))
+            make_edge1(t)
+            inverse = keep.tile([P, BLOCKS, P], F32, name="inverse%d" % (t - 1))
+            invert(inverse[:], size_sum)
+            make_edge2(t, act_up2)
+            make_score(t)
+            make_term2(t - 1)
+            term_sum = sum_terms(t - 1, score_up1, 0, BLOCKS, "num")
+            size_sum = sum_sizes(t, 0, BLOCKS)
+            make_hid(t - 1, 0, BLOCKS, term_sum, inverse)
+
+        halves = [(0, BLOCKS // 2), (BLOCKS // 2, BLOCKS)]
+        quantise(LAST + 2, nc.vector.tensor_copy)
+        act_up2 = fetch(act[LAST], up2_sb, "act_up2_%d" % LAST)
+        score_up1 = fetch(score[LAST - 1], up1_sb, "score_up1_%d" % (LAST - 1))
+        make_edge1(LAST)
+        inverse = keep.tile([P, BLOCKS, P], F32, name="inverse%d" % (LAST - 1))
+        invert(inverse[:], size_sum)
+        make_term2(LAST - 1)
+        term_sum = sum_terms(LAST - 1, score_up1, 0, BLOCKS, "num")
+        make_edge2(LAST, act_up2)
+        make_score(LAST)
+        size_sums = [sum_sizes(LAST, b0, b1) for b0, b1 in halves]
+        make_hid(LAST - 1, 0, BLOCKS, term_sum, inverse)
+        inverse = keep.tile([P, BLOCKS, P], F32, name="inverse%d" % LAST)
+        for (b0, b1), half_sum in zip(halves, size_sums):
+            invert(inverse[:, b0:b1, :], half_sum)
+        make_term2(LAST)
+
+        tail_tags = ["acc_w1", "acc_w2", "num", "num"]
+        term_sums = []
+        for step in range(BLOCKS + 2):
+            if step < BLOCKS:
+                score_up1 = score[LAST][:].indirect(up1_sb[:, step * LIST_COLS : (step + 1) * LIST_COLS])
+                term_sums.append(sum_terms(LAST, score_up1, step, step + 1, tail_tags[step]))
+            if 1 <= step <= BLOCKS:
+                make_hid(LAST, step - 1, step, term_sums[step - 1], inverse)
+            if step >= 2:
+                make_logits(step - 2)

from contextlib import ExitStack

import concourse.mybir as mybir
from concourse.masks import make_identity

K, T, S, N, H = 1024, 1024, 512, 128, 512
FLOPS = 2 * (2 * K * H * S + H * N * S)

F32 = mybir.dt.float32
BF16 = mybir.dt.bfloat16
I32 = mybir.dt.int32
U32 = mybir.dt.uint32
U16 = mybir.dt.uint16
U8 = mybir.dt.uint8
FP8X4 = mybir.dt.float8_e4m3fn_x4
ACT = mybir.ActivationFunctionType
MULT = mybir.AluOpType.mult

P = 128
PACK = 4
SLAB = PACK * P
PASSES = K // SLAB
TILES = H // P
LAST = TILES - 1
BLOCKS = S // P
LIST_COLS = P // 16
PAD = 32
SHIFT = 0.2
PSUM_BUFS = {"acc_w1": 1, "acc_w2": 1, "tot": 2, "num": 2, "back": 2}

GROUPS = (
    [[("w1", 0)], [("w1", 1)], [("w2", 0)]]
    + [[("w1", t + 1), ("w2", t)] for t in range(1, LAST)]
    + [[("w2", LAST), ("w3", 0)]]
)


def tile_picked_ytcoda_infl_p_kernel(
    tc, x_words, x_scales, w1, w2, vwa, vwb, unit, w3, offs, up1, up2, out
):
    nc = tc.nc
    with ExitStack() as ctx:
        keep = ctx.enter_context(tc.tile_pool(name="keep", bufs=1))
        ring = ctx.enter_context(tc.tile_pool(name="ring", bufs=2))
        psum = ctx.enter_context(tc.psum_pool(name="psum", bufs=1))

        def bank(tag, shape):
            return psum.tile(shape, F32, name=tag, bufs=PSUM_BUFS[tag])

        offs_sb = keep.tile([P, S // 16], U16, name="offs_sb")
        up1_sb = keep.tile([P, S // 16], U16, name="up1_sb")
        up2_sb = keep.tile([P, S // 16], U16, name="up2_sb")
        word_table = [keep.tile([P, T], U32, name="word_table%d" % g, align_bytes=64) for g in range(PASSES)]
        scale_table = keep.tile([P, T], U8, name="scale_table", align_bytes=64)
        x_codes = [keep.tile([P, S], U32, name="x_codes%d" % g, align_bytes=64) for g in range(PASSES)]
        x_bytes = keep.tile([P, S], U8, name="x_bytes", align_bytes=64)
        ident = keep.tile([P, P], F32, name="ident")
        unit_rows = keep.tile([P, P], F32, name="unit_rows")
        unit_sb = keep.tile([P, TILES], F32, name="unit_sb")
        vwa_sb = [keep.tile([P, S], F32, name="vwa%d" % t) for t in range(TILES)]
        vwb_sb = [keep.tile([P, S], F32, name="vwb%d" % t) for t in range(TILES)]
        act = [keep.tile([P, S + PAD], F32, name="act%d" % t) for t in range(TILES)]
        score = [keep.tile([P, S + PAD], F32, name="score%d" % t) for t in range(TILES)]
        hid_turned = keep.tile([P, BLOCKS, H], BF16, name="hid_turned", align_bytes=64)

        weights = {"w1": w1, "w2": w2, "w3": w3}
        raw, w_codes, w_bytes, place = [], [], [], {}
        for n, group in enumerate(GROUPS):
            slabs = 0
            for name, t in group:
                place[name, t] = (n, slabs)
                slabs = slabs + weights[name].shape[0] // SLAB
            raw.append(keep.tile([P, slabs, SLAB], F32, name="raw_%d" % n, align_bytes=64))
            w_codes.append(keep.tile([P, slabs * P], U32, name="w_codes%d" % n, align_bytes=64))
            w_bytes.append(keep.tile([P, slabs * P], U8, name="w_bytes%d" % n, align_bytes=64))

        def spent(name, t):
            n, s0 = place[name, t]
            return raw[n][:, s0 : s0 + PASSES, :]

        edge = [spent("w1", t + 1) for t in range(LAST)] + [spent("w2", LAST)]
        term = [spent("w2", 1), spent("w2", 2), spent("w1", 0), spent("w2", 0)]

        nc.gpsimd.memset(scale_table[:].bitcast(I32), 0)
        nc.gpsimd.memset(unit_rows[:], 0.0)
        warm = keep.tile([P, 2], F32, name="warm")
        nc.gpsimd.memset(warm[:, 0:1], 1.0)
        nc.scalar.activation(warm[:, 1:2], warm[:, 0:1], ACT.Abs_reciprocal_sqrt)

        def load_words(g):
            words = x_words[g].rearrange("p n r -> p (n r)").bitcast(I32)
            nc.sync.dma_start(out=word_table[g][:].bitcast(I32), in_=words)

        def load_scales():
            for q in range(4):
                rows = x_scales[:, 4 * q : 4 * q + 4, :].bitcast(I32)
                nc.sync.dma_start(out=scale_table[32 * q : 32 * q + 4 * PASSES, :].bitcast(I32), in_=rows)

        def load_weight(name, t):
            n, s0 = place[name, t]
            for g in range(weights[name].shape[0] // SLAB):
                rows = weights[name][g * SLAB : (g + 1) * SLAB, t * P : (t + 1) * P]
                nc.sync.dma_start(
                    out=raw[n][:, s0 + g, :].rearrange("p (r c) -> p r c", r=PACK),
                    in_=rows.rearrange("(p r) c -> p r c", r=PACK),
                )

        def load_rows(dst, src, t):
            nc.sync.dma_start(out=dst[t][:], in_=src[t * P : (t + 1) * P, :])

        nc.sync.dma_start(offs_sb[:], offs)
        load_words(0)
        load_scales()
        load_weight("w1", 0)
        load_words(1)
        nc.sync.dma_start(up1_sb[:], up1)
        nc.sync.dma_start(up2_sb[:], up2)
        load_weight("w1", 1)
        load_rows(vwa_sb, vwa, 0)
        nc.sync.dma_start(out=unit_rows[0:TILES, :], in_=unit.rearrange("(t p) o -> t (p o)", p=P))
        load_weight("w2", 0)
        load_rows(vwb_sb, vwb, 0)
        for t in range(1, TILES):
            for name, tile in GROUPS[t + 2]:
                load_weight(name, tile)
            load_rows(vwa_sb, vwa, t)
            load_rows(vwb_sb, vwb, t)

        make_identity(nc, ident[:])
        for t in range(TILES):
            nc.gpsimd.memset(act[t][:, S:], 0.0)
            nc.gpsimd.memset(score[t][:, S:], 0.0)

        def pick(dst, table):
            nc.vector.tensor_copy(dst[:], table[:].indirect(offs_sb[:]))

        def quantise(n, copy, pieces=1):
            slabs = raw[n].shape[1]
            grouped = keep.tile([P, slabs, SLAB], BF16, name="grouped%d" % n, align_bytes=64)
            step = slabs // pieces
            for s0 in range(0, slabs, step):
                copy(
                    grouped[:, s0 : s0 + step, :].rearrange("p s (c i r) -> p s c r i", i=4, r=PACK),
                    raw[n][:, s0 : s0 + step, :].rearrange("p s (r c i) -> p s c r i", i=4, r=PACK),
                )
            nc.vector.quantize_mx(
                out=w_codes[n][:].bitcast(FP8X4), scales=w_bytes[n][:], in_=grouped[:].rearrange("p s e -> p (s e)")
            )

        def stationary(name, t, g):
            n, s0 = place[name, t]
            cols = slice((s0 + g) * P, (s0 + g + 1) * P)
            return {"lhsT": w_codes[n][:, cols].bitcast(FP8X4), "lhsT_scale": w_bytes[n][:, cols]}

        def product(name, t):
            acc = bank("acc_" + name, [P, S])
            for g in range(PASSES):
                nc.tensor.matmul_mx(
                    out=acc[:],
                    rhs=x_codes[g][:].bitcast(FP8X4),
                    rhs_scale=x_bytes[4 * g :, :],
                    start=(g == 0),
                    stop=(g == PASSES - 1),
                    **stationary(name, t, g),
                )
            return acc

        def make_act(t):
            nc.scalar.activation(act[t][:, :S], product("w1", t)[:], ACT.Relu, bias=-SHIFT)

        def make_score(t):
            nc.scalar.activation(score[t][:, :S], product("w2", t)[:], ACT.Copy, scale=unit_sb[:, t : t + 1])

        def turn_unit():
            turned = bank("back", [P, P])
            nc.tensor.transpose(turned[:], unit_rows[:], ident[:])
            nc.scalar.copy(unit_sb[:], turned[:, 0:TILES])

        def fetch(window, order, name):
            fetched = keep.tile([P, S], F32, name=name)
            nc.scalar.activation(fetched[:], window[:].indirect(order[:]), ACT.Copy)
            return fetched[:]

        def add_turned(tag, pair, blocks):
            total = bank(tag, [P, blocks, P])
            for b in range(blocks):
                for e in range(2):
                    nc.tensor.matmul(
                        total[:, b, :],
                        lhsT=pair[:, e, b * P : (b + 1) * P],
                        rhs=ident[:],
                        start=(e == 0),
                        stop=(e == 1),
                        is_transpose=True,
                    )
            return total

        def make_edge1(t):
            nc.vector.tensor_tensor(edge[t][:, 0, :], act[t][:].indirect(up1_sb[:]), vwa_sb[t][:], MULT)

        def make_edge2(t, act_up2):
            nc.vector.tensor_tensor(edge[t][:, 1, :], act_up2, vwb_sb[t][:], MULT)

        def sum_sizes(t, b0, b1):
            sizes = ring.tile([P, 2, (b1 - b0) * P], F32, name="sizes")
            nc.scalar.activation(sizes[:], edge[t][:, :, b0 * P : b1 * P], ACT.Abs)
            return add_turned("tot", sizes, b1 - b0)

        def invert(inverse, size_sum):
            square = ring.tile([P, size_sum.shape[1] * P], F32, name="square")
            nc.scalar.activation(square[:], size_sum[:].rearrange("p b i -> p (b i)"), ACT.Square, bias=SHIFT)
            nc.scalar.activation(inverse.rearrange("p b i -> p (b i)"), square[:], ACT.Abs_reciprocal_sqrt)

        def make_term2(t):
            nc.vector.tensor_tensor(term[t][:, 1, :], score[t][:, :S], edge[t][:, 1, :], MULT)

        def sum_terms(t, score_up1, b0, b1, tag):
            cols = slice(b0 * P, b1 * P)
            nc.vector.tensor_tensor(term[t][:, 0, cols], score_up1, edge[t][:, 0, cols], MULT)
            return add_turned(tag, term[t][:, :, cols], b1 - b0)

        def make_hid(t, b0, b1, term_sum, inverse):
            nc.vector.tensor_tensor(hid_turned[:, b0:b1, t * P : (t + 1) * P], term_sum[:], inverse[:, b0:b1, :], MULT)

        def make_logits(b):
            pairs = hid_turned[:].bitcast(F32)
            back = bank("back", [P, 1, 2, P])
            for u in range(2):
                nc.tensor.transpose(back[:, 0, u, :], pairs[:, b, u : H // 2 : 2], ident[:])
            grouped = keep.tile([P, P, PACK], BF16, name="hid_grouped%d" % b, align_bytes=64)
            nc.scalar.copy(
                grouped[:].bitcast(F32).rearrange("p (o j) u -> p o j u", o=1), back[:].rearrange("p o u j -> p o j u")
            )
            hid_codes = keep.tile([P, P], U32, name="hid_codes%d" % b, align_bytes=64)
            hid_bytes = keep.tile([P, P], U8, name="hid_bytes%d" % b, align_bytes=64)
            nc.vector.quantize_mx(
                out=hid_codes[:].bitcast(FP8X4), scales=hid_bytes[:], in_=grouped[:].rearrange("p j r -> p (j r)")
            )
            acc = bank("tot", [P, S])
            nc.tensor.matmul_mx(
                out=acc[:, :P],
                rhs=hid_codes[:].bitcast(FP8X4),
                rhs_scale=hid_bytes[:],
                start=True,
                stop=True,
                **stationary("w3", 0, 0),
            )
            result = keep.tile([P, P], F32, name="result%d" % b)
            nc.scalar.copy(result[:], acc[:, :P])
            nc.sync.dma_start(out=out[:, b * P : (b + 1) * P], in_=result[:])

        pick(x_codes[0], word_table[0])
        pick(x_bytes, scale_table)
        quantise(0, nc.scalar.copy, pieces=PASSES)
        pick(x_codes[1], word_table[1])
        make_act(0)
        turn_unit()

        quantise(1, nc.vector.tensor_copy)
        act_up2 = fetch(act[0], up2_sb, "act_up2_0")
        make_act(1)
        make_edge1(0)
        quantise(2, nc.vector.tensor_copy)
        make_edge2(0, act_up2)
        make_score(0)
        size_sum = sum_sizes(0, 0, BLOCKS)

        for t in range(1, LAST):
            quantise(t + 2, nc.vector.tensor_copy)
            act_up2 = fetch(act[t], up2_sb, "act_up2_%d" % t)
            make_act(t + 1)
            score_up1 = fetch(score[t - 1], up1_sb, "score_up1_%d" % (t - 1))
            make_edge1(t)
            inverse = keep.tile([P, BLOCKS, P], F32, name="inverse%d" % (t - 1))
            invert(inverse[:], size_sum)
            make_edge2(t, act_up2)
            make_score(t)
            make_term2(t - 1)
            term_sum = sum_terms(t - 1, score_up1, 0, BLOCKS, "num")
            size_sum = sum_sizes(t, 0, BLOCKS)
            make_hid(t - 1, 0, BLOCKS, term_sum, inverse)

        halves = [(0, BLOCKS // 2), (BLOCKS // 2, BLOCKS)]
        quantise(LAST + 2, nc.vector.tensor_copy)
        act_up2 = fetch(act[LAST], up2_sb, "act_up2_%d" % LAST)
        score_up1 = fetch(score[LAST - 1], up1_sb, "score_up1_%d" % (LAST - 1))
        make_edge1(LAST)
        inverse = keep.tile([P, BLOCKS, P], F32, name="inverse%d" % (LAST - 1))
        invert(inverse[:], size_sum)
        make_term2(LAST - 1)
        term_sum = sum_terms(LAST - 1, score_up1, 0, BLOCKS, "num")
        make_edge2(LAST, act_up2)
        make_score(LAST)
        size_sums = [sum_sizes(LAST, b0, b1) for b0, b1 in halves]
        make_hid(LAST - 1, 0, BLOCKS, term_sum, inverse)
        inverse = keep.tile([P, BLOCKS, P], F32, name="inverse%d" % LAST)
        for (b0, b1), half_sum in zip(halves, size_sums):
            invert(inverse[:, b0:b1, :], half_sum)
        make_term2(LAST)

        tail_tags = ["acc_w1", "acc_w2", "num", "num"]
        term_sums = []
        for step in range(BLOCKS + 2):
            if step < BLOCKS:
                score_up1 = score[LAST][:].indirect(up1_sb[:, step * LIST_COLS : (step + 1) * LIST_COLS])
                term_sums.append(sum_terms(LAST, score_up1, step, step + 1, tail_tags[step]))
            if 1 <= step <= BLOCKS:
                make_hid(LAST, step - 1, step, term_sums[step - 1], inverse)
            if step >= 2:
                make_logits(step - 2)
